import numpy as np
import ml_dtypes

BF16 = ml_dtypes.bfloat16


def bf(x):
    return np.asarray(x, np.float32).astype(BF16)


def f32(x):
    return np.asarray(x, np.float32)


def f64(x):
    return np.asarray(x).astype(np.float64)


def striped(idx):
    return np.tile(idx.reshape(-1, 16).T, (8, 1))


S, K, M, N, E, Q = 512, 128, 128, 256, 4, 64


def gelu_tanh(v):
    return 0.5 * v * (1.0 + np.tanh(np.sqrt(2.0 / np.pi) * (v + 0.044715 * v**3)))


def setup_inputs():
    return {"base": bf(np.random.standard_normal((M, S))), "x": bf(np.random.standard_normal((K, N))), "w": bf(np.random.standard_normal((E, K, M)) / np.sqrt(K)), "b": f32(0.5 * np.random.standard_normal((M, 1))), "offs": striped(np.random.permutation(S)[:N])}


def reference(base, x, w, b, offs):
    idx = offs[:16].T.reshape(-1)
    z = f64(base).copy()
    for e in range(E):
        z[:, idx[e * Q : (e + 1) * Q]] = f64(w)[e].T @ f64(x)[:, e * Q : (e + 1) * Q]
    return gelu_tanh(z + f64(b))

@@ -1,0 +1,52 @@
+import concourse.mybir as mybir
+from concourse.masks import make_identity
+
+BF16, F32, U16 = mybir.dt.bfloat16, mybir.dt.float32, mybir.dt.uint16
+GELU_TANH = mybir.ActivationFunctionType.Gelu_apprx_tanh
+
+M, K = 128, 128
+S = 512
+N = 256
+E = 4
+Q = N // E
+OFFSET_COLUMNS = Q // 16
+
+FLOPS = 2 * K * M * N
+
+
+def tile_scatter_matmul_kernel(tc, base, x, w, b, offs, out):
+    nc = tc.nc
+    with (
+        tc.tile_pool(name="held", bufs=1) as held,
+        tc.psum_pool(name="psum", bufs=1) as psum,
+    ):
+        offsets = held.tile([128, N // 16], U16, name="offsets")
+        nc.sync.dma_start(offsets[:], offs)
+        base_sb = held.tile([M, S], BF16, name="base_sb")
+        nc.scalar.dma_start(base_sb[:], base)
+        w_sb = held.tile([K, E, M], BF16, name="w_sb")
+        nc.sync.dma_start(w_sb[:], w.rearrange("e k m -> k e m"))
+        x_sb = held.tile([K, N], BF16, name="x_sb")
+        nc.scalar.dma_start(x_sb[:], x)
+        bias = held.tile([M, 1], F32, name="bias")
+        nc.sync.dma_start(bias[:], b)
+
+        identity = held.tile([M, M], BF16, name="identity")
+        make_identity(nc, identity[:])
+
+        window = psum.tile([M, S], F32, name="window")
+        nc.tensor.matmul(window[:], identity[:], base_sb[:], start=True, stop=True)
+
+        for e in range(E):
+            piece = offsets[:, e * OFFSET_COLUMNS : (e + 1) * OFFSET_COLUMNS]
+            nc.tensor.matmul(
+                window[:].indirect(piece),
+                w_sb[:, e, :],
+                x_sb[:, e * Q : (e + 1) * Q],
+                start=True,
+                stop=True,
+            )
+
+        result = held.tile([M, S], F32, name="result")
+        nc.scalar.activation(result[:], window[:], GELU_TANH, bias=bias[:])
+        nc.sync.dma_start(out, result[:])

@@ -31,6 +31,10 @@ def tile_scatter_matmul_kernel(tc, base, x, w, b, offs, out):
         bias = held.tile([M, 1], F32, name="bias")
         nc.sync.dma_start(bias[:], b)
 
+        scrap = held.tile([M, 1], F32, name="scrap")
+        nc.vector.memset(scrap[:], 0.0)
+        nc.scalar.activation(scrap[:], scrap[:], GELU_TANH)
+
         identity = held.tile([M, M], BF16, name="identity")
         make_identity(nc, identity[:])
 

@@ -10,6 +10,7 @@ N = 256
 E = 4
 Q = N // E
 OFFSET_COLUMNS = Q // 16
+HALVES = 2
 
 FLOPS = 2 * K * M * N
 
@@ -52,5 +53,7 @@ def tile_scatter_matmul_kernel(tc, base, x, w, b, offs, out):
             )
 
         result = held.tile([M, S], F32, name="result")
-        nc.scalar.activation(result[:], window[:], GELU_TANH, bias=bias[:])
-        nc.sync.dma_start(out, result[:])
+        for h in range(HALVES):
+            columns = slice(h * S // HALVES, (h + 1) * S // HALVES)
+            nc.scalar.activation(result[:, columns], window[:, columns], GELU_TANH, bias=bias[:])
+            nc.sync.dma_start(out[:, columns], result[:, columns])

@@ -10,7 +10,7 @@ N = 256
 E = 4
 Q = N // E
 OFFSET_COLUMNS = Q // 16
-HALVES = 2
+WARMING_MATMULS = 3
 
 FLOPS = 2 * K * M * N
 
@@ -32,9 +32,15 @@ def tile_scatter_matmul_kernel(tc, base, x, w, b, offs, out):
         bias = held.tile([M, 1], F32, name="bias")
         nc.sync.dma_start(bias[:], b)
 
+        zeros = held.tile([K, S], BF16, name="zeros")
+        nc.vector.memset(zeros[:], 0.0)
+
         scrap = held.tile([M, 1], F32, name="scrap")
-        nc.vector.memset(scrap[:], 0.0)
-        nc.scalar.activation(scrap[:], scrap[:], GELU_TANH)
+        nc.scalar.activation(scrap[:], zeros[:, 0:1], GELU_TANH)
+
+        unread = psum.tile([M, S], F32, name="unread")
+        for i in range(WARMING_MATMULS):
+            nc.tensor.matmul(unread[:], zeros[:, 0:M], zeros[:], start=True, stop=True)
 
         identity = held.tile([M, M], BF16, name="identity")
         make_identity(nc, identity[:])
@@ -53,7 +59,5 @@ def tile_scatter_matmul_kernel(tc, base, x, w, b, offs, out):
             )
 
         result = held.tile([M, S], F32, name="result")
-        for h in range(HALVES):
-            columns = slice(h * S // HALVES, (h + 1) * S // HALVES)
-            nc.scalar.activation(result[:, columns], window[:, columns], GELU_TANH, bias=bias[:])
-            nc.sync.dma_start(out[:, columns], result[:, columns])
+        nc.scalar.activation(result[:], window[:], GELU_TANH, bias=bias[:])
+        nc.sync.dma_start(out, result[:])

@@ -10,7 +10,7 @@ N = 256
 E = 4
 Q = N // E
 OFFSET_COLUMNS = Q // 16
-WARMING_MATMULS = 3
+WARMING_MATMULS = 12
 
 FLOPS = 2 * K * M * N
 
@@ -32,15 +32,15 @@ def tile_scatter_matmul_kernel(tc, base, x, w, b, offs, out):
         bias = held.tile([M, 1], F32, name="bias")
         nc.sync.dma_start(bias[:], b)
 
-        zeros = held.tile([K, S], BF16, name="zeros")
+        zeros = held.tile([K, M], BF16, name="zeros")
         nc.vector.memset(zeros[:], 0.0)
 
         scrap = held.tile([M, 1], F32, name="scrap")
         nc.scalar.activation(scrap[:], zeros[:, 0:1], GELU_TANH)
 
-        unread = psum.tile([M, S], F32, name="unread")
+        unread = psum.tile([M, M], F32, name="unread")
         for i in range(WARMING_MATMULS):
-            nc.tensor.matmul(unread[:], zeros[:, 0:M], zeros[:], start=True, stop=True)
+            nc.tensor.matmul(unread[:], zeros[:], zeros[:], start=True, stop=True)
 
         identity = held.tile([M, M], BF16, name="identity")
         make_identity(nc, identity[:])

@@ -10,6 +10,7 @@ N = 256
 E = 4
 Q = N // E
 OFFSET_COLUMNS = Q // 16
+BLOCK = 32
 WARMING_MATMULS = 12
 
 FLOPS = 2 * K * M * N
@@ -21,6 +22,9 @@ def tile_scatter_matmul_kernel(tc, base, x, w, b, offs, out):
         tc.tile_pool(name="held", bufs=1) as held,
         tc.psum_pool(name="psum", bufs=1) as psum,
     ):
+        zeros = held.tile([K, M], BF16, name="zeros")
+        nc.vector.memset(zeros[:], 0.0)
+
         offsets = held.tile([128, N // 16], U16, name="offsets")
         nc.sync.dma_start(offsets[:], offs)
         base_sb = held.tile([M, S], BF16, name="base_sb")
@@ -29,11 +33,10 @@ def tile_scatter_matmul_kernel(tc, base, x, w, b, offs, out):
         nc.sync.dma_start(w_sb[:], w.rearrange("e k m -> k e m"))
         x_sb = held.tile([K, N], BF16, name="x_sb")
         nc.scalar.dma_start(x_sb[:], x)
-        bias = held.tile([M, 1], F32, name="bias")
-        nc.sync.dma_start(bias[:], b)
 
-        zeros = held.tile([K, M], BF16, name="zeros")
-        nc.vector.memset(zeros[:], 0.0)
+        bias_rows = held.tile([M, BLOCK], F32, name="bias_rows", align_bytes=64)
+        nc.gpsimd.memset(bias_rows[:], 0.0)
+        nc.sync.dma_start(bias_rows[0:M:BLOCK, :], b.rearrange("(q i) o -> q (i o)", i=BLOCK))
 
         scrap = held.tile([M, 1], F32, name="scrap")
         nc.scalar.activation(scrap[:], zeros[:, 0:1], GELU_TANH)
@@ -58,6 +61,10 @@ def tile_scatter_matmul_kernel(tc, base, x, w, b, offs, out):
                 stop=True,
             )
 
+        bias_columns = held.tile([M, BLOCK], F32, name="bias_columns", align_bytes=64)
+        nc.vector.transpose(bias_columns[:], bias_rows[:])
+        bias = bias_columns[:, 0:1]
+
         result = held.tile([M, S], F32, name="result")
-        nc.scalar.activation(result[:], window[:], GELU_TANH, bias=bias[:])
+        nc.scalar.activation(result[:], window[:], GELU_TANH, bias=bias)
         nc.sync.dma_start(out, result[:])

@@ -25,18 +25,19 @@ def tile_scatter_matmul_kernel(tc, base, x, w, b, offs, out):
         zeros = held.tile([K, M], BF16, name="zeros")
         nc.vector.memset(zeros[:], 0.0)
 
+        base_sb = held.tile([M, S], BF16, name="base_sb")
+        nc.sync.dma_start(base_sb[:], base)
         offsets = held.tile([128, N // 16], U16, name="offsets")
         nc.sync.dma_start(offsets[:], offs)
-        base_sb = held.tile([M, S], BF16, name="base_sb")
-        nc.scalar.dma_start(base_sb[:], base)
-        w_sb = held.tile([K, E, M], BF16, name="w_sb")
-        nc.sync.dma_start(w_sb[:], w.rearrange("e k m -> k e m"))
         x_sb = held.tile([K, N], BF16, name="x_sb")
-        nc.scalar.dma_start(x_sb[:], x)
+        nc.sync.dma_start(x_sb[:], x)
+        w_sb = [held.tile([K, M], BF16, name="w_sb%d" % e) for e in range(E)]
+        for e in range(E):
+            nc.sync.dma_start(w_sb[e][:], w[e, :, :])
 
         bias_rows = held.tile([M, BLOCK], F32, name="bias_rows", align_bytes=64)
-        nc.gpsimd.memset(bias_rows[:], 0.0)
-        nc.sync.dma_start(bias_rows[0:M:BLOCK, :], b.rearrange("(q i) o -> q (i o)", i=BLOCK))
+        nc.vector.memset(bias_rows[:], 0.0)
+        nc.scalar.dma_start(bias_rows[0:M:BLOCK, :], b.rearrange("(q i) o -> q (i o)", i=BLOCK))
 
         scrap = held.tile([M, 1], F32, name="scrap")
         nc.scalar.activation(scrap[:], zeros[:, 0:1], GELU_TANH)
@@ -46,7 +47,8 @@ def tile_scatter_matmul_kernel(tc, base, x, w, b, offs, out):
             nc.tensor.matmul(unread[:], zeros[:], zeros[:], start=True, stop=True)
 
         identity = held.tile([M, M], BF16, name="identity")
-        make_identity(nc, identity[:])
+        nc.vector.memset(identity[:], 0.0)
+        make_identity(nc, identity[:], nomemset=True)
 
         window = psum.tile([M, S], F32, name="window")
         nc.tensor.matmul(window[:], identity[:], base_sb[:], start=True, stop=True)
@@ -55,7 +57,7 @@ def tile_scatter_matmul_kernel(tc, base, x, w, b, offs, out):
             piece = offsets[:, e * OFFSET_COLUMNS : (e + 1) * OFFSET_COLUMNS]
             nc.tensor.matmul(
                 window[:].indirect(piece),
-                w_sb[:, e, :],
+                w_sb[e][:],
                 x_sb[:, e * Q : (e + 1) * Q],
                 start=True,
                 stop=True,

@@ -31,9 +31,9 @@ def tile_scatter_matmul_kernel(tc, base, x, w, b, offs, out):
         nc.sync.dma_start(offsets[:], offs)
         x_sb = held.tile([K, N], BF16, name="x_sb")
         nc.sync.dma_start(x_sb[:], x)
-        w_sb = [held.tile([K, M], BF16, name="w_sb%d" % e) for e in range(E)]
-        for e in range(E):
-            nc.sync.dma_start(w_sb[e][:], w[e, :, :])
+        w_sb = [held.tile([K, 2, M], BF16, name="w_sb%d" % pair) for pair in range(E // 2)]
+        for pair in range(E // 2):
+            nc.sync.dma_start(w_sb[pair][:], w[2 * pair : 2 * pair + 2, :, :].rearrange("e k m -> k e m"))
 
         bias_rows = held.tile([M, BLOCK], F32, name="bias_rows", align_bytes=64)
         nc.vector.memset(bias_rows[:], 0.0)
@@ -57,7 +57,7 @@ def tile_scatter_matmul_kernel(tc, base, x, w, b, offs, out):
             piece = offsets[:, e * OFFSET_COLUMNS : (e + 1) * OFFSET_COLUMNS]
             nc.tensor.matmul(
                 window[:].indirect(piece),
-                w_sb[e][:],
+                w_sb[e // 2][:, e % 2, :],
                 x_sb[:, e * Q : (e + 1) * Q],
                 start=True,
                 stop=True,

@@ -12,6 +12,7 @@ Q = N // E
 OFFSET_COLUMNS = Q // 16
 BLOCK = 32
 WARMING_MATMULS = 12
+DMA_ALIGN = 256
 
 FLOPS = 2 * K * M * N
 
@@ -25,13 +26,13 @@ def tile_scatter_matmul_kernel(tc, base, x, w, b, offs, out):
         zeros = held.tile([K, M], BF16, name="zeros")
         nc.vector.memset(zeros[:], 0.0)
 
-        base_sb = held.tile([M, S], BF16, name="base_sb")
+        base_sb = held.tile([M, S], BF16, name="base_sb", align_bytes=DMA_ALIGN)
         nc.sync.dma_start(base_sb[:], base)
         offsets = held.tile([128, N // 16], U16, name="offsets")
         nc.sync.dma_start(offsets[:], offs)
-        x_sb = held.tile([K, N], BF16, name="x_sb")
+        x_sb = held.tile([K, N], BF16, name="x_sb", align_bytes=DMA_ALIGN)
         nc.sync.dma_start(x_sb[:], x)
-        w_sb = [held.tile([K, 2, M], BF16, name="w_sb%d" % pair) for pair in range(E // 2)]
+        w_sb = [held.tile([K, 2, M], BF16, name="w_sb%d" % pair, align_bytes=DMA_ALIGN) for pair in range(E // 2)]
         for pair in range(E // 2):
             nc.sync.dma_start(w_sb[pair][:], w[2 * pair : 2 * pair + 2, :, :].rearrange("e k m -> k e m"))
 
@@ -67,6 +68,6 @@ def tile_scatter_matmul_kernel(tc, base, x, w, b, offs, out):
         nc.vector.transpose(bias_columns[:], bias_rows[:])
         bias = bias_columns[:, 0:1]
 
-        result = held.tile([M, S], F32, name="result")
+        result = held.tile([M, S], F32, name="result", align_bytes=DMA_ALIGN)
         nc.scalar.activation(result[:], window[:], GELU_TANH, bias=bias)
         nc.sync.dma_start(out, result[:])

@@ -26,10 +26,10 @@ def tile_scatter_matmul_kernel(tc, base, x, w, b, offs, out):
         zeros = held.tile([K, M], BF16, name="zeros")
         nc.vector.memset(zeros[:], 0.0)
 
-        base_sb = held.tile([M, S], BF16, name="base_sb", align_bytes=DMA_ALIGN)
-        nc.sync.dma_start(base_sb[:], base)
         offsets = held.tile([128, N // 16], U16, name="offsets")
         nc.sync.dma_start(offsets[:], offs)
+        base_sb = held.tile([M, S], BF16, name="base_sb", align_bytes=DMA_ALIGN)
+        nc.sync.dma_start(base_sb[:], base)
         x_sb = held.tile([K, N], BF16, name="x_sb", align_bytes=DMA_ALIGN)
         nc.sync.dma_start(x_sb[:], x)
         w_sb = [held.tile([K, 2, M], BF16, name="w_sb%d" % pair, align_bytes=DMA_ALIGN) for pair in range(E // 2)]

@@ -38,7 +38,7 @@ def tile_scatter_matmul_kernel(tc, base, x, w, b, offs, out):
 
         bias_rows = held.tile([M, BLOCK], F32, name="bias_rows", align_bytes=64)
         nc.vector.memset(bias_rows[:], 0.0)
-        nc.scalar.dma_start(bias_rows[0:M:BLOCK, :], b.rearrange("(q i) o -> q (i o)", i=BLOCK))
+        nc.sync.dma_start(bias_rows[0:M:BLOCK, :], b.rearrange("(q i) o -> q (i o)", i=BLOCK))
 
         scrap = held.tile([M, 1], F32, name="scrap")
         nc.scalar.activation(scrap[:], zeros[:, 0:1], GELU_TANH)

import concourse.mybir as mybir
from concourse.masks import make_identity

BF16, F32, U16 = mybir.dt.bfloat16, mybir.dt.float32, mybir.dt.uint16
GELU_TANH = mybir.ActivationFunctionType.Gelu_apprx_tanh

M, K = 128, 128
S = 512
N = 256
E = 4
Q = N // E
OFFSET_COLUMNS = Q // 16
BLOCK = 32
WARMING_MATMULS = 12
DMA_ALIGN = 256

FLOPS = 2 * K * M * N


def tile_scatter_matmul_kernel(tc, base, x, w, b, offs, out):
    nc = tc.nc
    with (
        tc.tile_pool(name="held", bufs=1) as held,
        tc.psum_pool(name="psum", bufs=1) as psum,
    ):
        zeros = held.tile([K, M], BF16, name="zeros")
        nc.vector.memset(zeros[:], 0.0)

        offsets = held.tile([128, N // 16], U16, name="offsets")
        nc.sync.dma_start(offsets[:], offs)
        base_sb = held.tile([M, S], BF16, name="base_sb", align_bytes=DMA_ALIGN)
        nc.sync.dma_start(base_sb[:], base)
        x_sb = held.tile([K, N], BF16, name="x_sb", align_bytes=DMA_ALIGN)
        nc.sync.dma_start(x_sb[:], x)
        w_sb = [held.tile([K, 2, M], BF16, name="w_sb%d" % pair, align_bytes=DMA_ALIGN) for pair in range(E // 2)]
        for pair in range(E // 2):
            nc.sync.dma_start(w_sb[pair][:], w[2 * pair : 2 * pair + 2, :, :].rearrange("e k m -> k e m"))

        bias_rows = held.tile([M, BLOCK], F32, name="bias_rows", align_bytes=64)
        nc.vector.memset(bias_rows[:], 0.0)
        nc.sync.dma_start(bias_rows[0:M:BLOCK, :], b.rearrange("(q i) o -> q (i o)", i=BLOCK))

        scrap = held.tile([M, 1], F32, name="scrap")
        nc.scalar.activation(scrap[:], zeros[:, 0:1], GELU_TANH)

        unread = psum.tile([M, M], F32, name="unread")
        for i in range(WARMING_MATMULS):
            nc.tensor.matmul(unread[:], zeros[:], zeros[:], start=True, stop=True)

        identity = held.tile([M, M], BF16, name="identity")
        nc.vector.memset(identity[:], 0.0)
        make_identity(nc, identity[:], nomemset=True)

        window = psum.tile([M, S], F32, name="window")
        nc.tensor.matmul(window[:], identity[:], base_sb[:], start=True, stop=True)

        for e in range(E):
            piece = offsets[:, e * OFFSET_COLUMNS : (e + 1) * OFFSET_COLUMNS]
            nc.tensor.matmul(
                window[:].indirect(piece),
                w_sb[e // 2][:, e % 2, :],
                x_sb[:, e * Q : (e + 1) * Q],
                start=True,
                stop=True,
            )

        bias_columns = held.tile([M, BLOCK], F32, name="bias_columns", align_bytes=64)
        nc.vector.transpose(bias_columns[:], bias_rows[:])
        bias = bias_columns[:, 0:1]

        result = held.tile([M, S], F32, name="result", align_bytes=DMA_ALIGN)
        nc.scalar.activation(result[:], window[:], GELU_TANH, bias=bias)
        nc.sync.dma_start(out, result[:])
